import numpy as np, ml_dtypes
CORES = [7,391,135,263,15,399,143,271]
N = 8
R, TK = 64, 128
def setup_inputs(rng):
    v = (rng.standard_normal((N, 128, R), dtype=np.float32) / np.float32(np.sqrt(128 * N))).astype(ml_dtypes.bfloat16)
    return {"x": rng.standard_normal((N, 128, TK), dtype=np.float32).astype(ml_dtypes.bfloat16), "v": v, "vt": v.transpose(0, 2, 1).copy()}
def setup_inputs_big(rng):
    d = setup_inputs(rng)
    for k in ("x",): d[k] = (d[k].astype(np.float32) * 1048576.0).astype(d[k].dtype)
    return d
def setup_inputs_small(rng):
    d = setup_inputs(rng)
    for k in ("x",): d[k] = (d[k].astype(np.float32) * (1 / 1048576.0)).astype(d[k].dtype)
    return d
def setup_inputs_apart(rng):
    d = setup_inputs(rng)
    f = (10.0 ** rng.permutation(np.linspace(-1.5, 1.5, N))).astype(np.float32).reshape(N, 1, 1)
    for k in ("x",): d[k] = (d[k].astype(np.float32) * f).astype(d[k].dtype)
    return d
def reference(x, v, vt):
    X, V, VT = x.astype(np.float64), v.astype(np.float64), vt.astype(np.float64)
    t = sum(V[j].T @ X[j] for j in range(N))
    return {"y": np.stack([X[r] - 2.0 * (VT[r].T @ t) for r in range(N)]).astype(ml_dtypes.bfloat16)}

@@ -1,0 +1,101 @@
+from concourse.bass import DstId, RemoteDMATransfer
+from concourse.mybir import AluOpType
+
+HALF = 64
+
+SCRATCH = {
+    "xs": ("sbuf", [128, 128], "bfloat16"),
+    "w": ("sbuf", [128, 192], "bfloat16"),
+    "vraw": ("sbuf", [128, 128], "bfloat16"),
+    "va": ("sbuf", [128, 128], "bfloat16"),
+    "vb": ("sbuf", [128, 128], "bfloat16"),
+    "p": ("sbuf", [128, HALF], "bfloat16"),
+    "land": ("sbuf", [128, 3 * HALF], "bfloat16"),
+    "far": ("sbuf", [128, HALF], "bfloat16"),
+    "e": ("sbuf", [128, 128], "float32"),
+    "ys": ("sbuf", [128, 128], "bfloat16"),
+    "pt": ("psum", [128, 512], "float32"),
+    "pe": ("psum", [128, 512], "float32"),
+    "pf": ("psum", [128, 512], "float32"),
+}
+SEMAPHORES = ["ld", "ldv", "z", "zv", "mt", "pr", "vd", "a1", "a2", "snt", "me", "ed", "mf", "yr", "st"]
+
+
+def rank_program(g, core, T, topo):
+    if T.rank_of(core) is None:
+        return
+    S = T.sem
+    top, bot = slice(0, HALF), slice(HALF, 2 * HALF)
+
+    peers = [d for d in T.cores if d != core]
+    near = [d for d in peers if topo.rack(topo.host(d)) == topo.rack(topo.host(core))]
+    cabled = [d for d in peers if d not in near and topo.may_write(core, d) and topo.chip(d) == topo.chip(core)][0]
+
+    def slot(a, b):
+        k = 0 if topo.mates(a, b) else (1 if topo.same_plane(a, b) else 2)
+        return T.land[:, k * HALF:(k + 1) * HALF]
+
+    def dst_id(d):
+        rid, pid = topo.addr(d, core)
+        return DstId(rid=rid, pnc=pid)
+
+    def n_engines(mask):
+        return bin(mask).count("1")
+
+    mask1 = topo.mask(core, near[0]) & topo.mask(core, near[1]) & topo.mask(core, near[2])
+    mask2 = topo.mask(core, cabled)
+
+    g.sync.dma_start(T.xs[:], T.x[:]).then_inc(S.ld, 16)
+    g.scalar.dma_start(T.w[:, HALF:2 * HALF], T.v[:]).then_inc(S.ld, 16)
+    g.sync.dma_start(T.vraw[top, :], T.vt[:]).then_inc(S.ldv, 16)
+    g.scalar.dma_start(T.vraw[bot, :], T.vt[:]).then_inc(S.ldv, 16)
+    g.vector.memset(T.w[:, 0:HALF], 0.0).then_inc(S.z, 1)
+    g.vector.memset(T.w[:, 2 * HALF:3 * HALF], 0.0).then_inc(S.z, 1)
+    g.vector.memset(T.va[bot, :], 0.0).then_inc(S.zv, 1)
+    g.vector.memset(T.vb[top, :], 0.0).then_inc(S.zv, 1)
+
+    g.tensor.wait_ge(S.z, 2)
+    g.tensor.wait_ge(S.ld, 32)
+    g.tensor.matmul(T.pt[:, 0:HALF], T.w[:, HALF:3 * HALF], T.xs[:, top], True, False)
+    g.tensor.matmul(T.pt[:, 0:HALF], T.w[:, 0:2 * HALF], T.xs[:, bot], False, True).then_inc(S.mt, 1)
+    g.vector.wait_ge(S.mt, 1)
+    g.vector.tensor_copy(T.p[:], T.pt[:, 0:HALF]).then_inc(S.pr, 1)
+
+    g.wait_ge(S.pr, 1)
+    g.remote_dma_fused([RemoteDMATransfer(
+        dst_ids=[dst_id(d) for d in near], dma_engine_mask=mask1, remote_sem=S.a1,
+        srcs=[T.p[:]], dsts=[slot(core, d) for d in near], alu_op=0)], local_sem=S.snt)
+
+    g.vector.wait_ge(S.ldv, 32)
+    g.vector.tensor_tensor(T.va[top, :], T.vraw[top, :], T.vraw[top, :], AluOpType.add).then_inc(S.vd, 1)
+    g.vector.tensor_tensor(T.vb[bot, :], T.vraw[bot, :], T.vraw[bot, :], AluOpType.add).then_inc(S.vd, 1)
+
+    mine = [T.p[:]] + [slot(d, core) for d in near]
+    g.wait_ge(S.a1, 3 * n_engines(mask1))
+    g.remote_dma_fused([RemoteDMATransfer(
+        dst_ids=[dst_id(cabled)], dma_engine_mask=mask2, remote_sem=S.a2,
+        srcs=mine, dsts=[T.far[:]], alu_op=1)], local_sem=S.snt)
+
+    g.tensor.wait_ge(S.pr, 1)
+    g.tensor.wait_ge(S.zv, 2)
+    g.tensor.wait_ge(S.vd, 2)
+    g.tensor.wait_ge(S.a1, 3 * n_engines(mask1))
+    for half, stat in ((top, T.va), (bot, T.vb)):
+        for i, src in enumerate(mine):
+            mm = g.tensor.matmul(T.pe[:, half], stat[:], src, i == 0, i == len(mine) - 1)
+        mm.then_inc(S.me, 1)
+    g.vector.wait_ge(S.ld, 32)
+    g.vector.wait_ge(S.me, 2)
+    g.vector.tensor_tensor(T.e[:], T.xs[:], T.pe[:, 0:2 * HALF], AluOpType.subtract).then_inc(S.ed, 1)
+
+    g.tensor.wait_ge(S.a2, n_engines(mask2))
+    for half, stat in ((top, T.va), (bot, T.vb)):
+        g.tensor.matmul(T.pf[:, half], stat[:], T.far[:], True, True).then_inc(S.mf, 1)
+    g.vector.wait_ge(S.ed, 1)
+    g.vector.wait_ge(S.mf, 2)
+    g.vector.tensor_tensor(T.ys[:], T.e[:], T.pf[:, 0:2 * HALF], AluOpType.subtract).then_inc(S.yr, 1)
+    g.sync.wait_ge(S.yr, 1)
+    g.sync.dma_start(T.y[:], T.ys[:]).then_inc(S.st, 16)
+    g.sync.wait_ge(S.st, 16)
+
+    g.wait_ge(S.snt, n_engines(mask1) + n_engines(mask2))

@@ -10,15 +10,14 @@ SCRATCH = {
     "va": ("sbuf", [128, 128], "bfloat16"),
     "vb": ("sbuf", [128, 128], "bfloat16"),
     "p": ("sbuf", [128, HALF], "bfloat16"),
-    "land": ("sbuf", [128, 3 * HALF], "bfloat16"),
+    "land": ("sbuf", [128, 4 * HALF], "bfloat16"),
     "far": ("sbuf", [128, HALF], "bfloat16"),
-    "e": ("sbuf", [128, 128], "float32"),
     "ys": ("sbuf", [128, 128], "bfloat16"),
     "pt": ("psum", [128, 512], "float32"),
-    "pe": ("psum", [128, 512], "float32"),
-    "pf": ("psum", [128, 512], "float32"),
+    "pe0": ("psum", [128, 512], "float32"),
+    "pe1": ("psum", [128, 512], "float32"),
 }
-SEMAPHORES = ["ld", "ldv", "z", "zv", "mt", "pr", "vd", "a1", "a2", "snt", "me", "ed", "mf", "yr", "st"]
+SEMAPHORES = ["ld", "ldv", "z", "zv", "mt", "pr", "vd", "a1", "ai", "a2", "snt", "mf0", "mf1", "yr", "st"]
 
 
 def rank_program(g, core, T, topo):
@@ -29,21 +28,27 @@ def rank_program(g, core, T, topo):
 
     peers = [d for d in T.cores if d != core]
     near = [d for d in peers if topo.rack(topo.host(d)) == topo.rack(topo.host(core))]
-    cabled = [d for d in peers if d not in near and topo.may_write(core, d) and topo.chip(d) == topo.chip(core)][0]
-
-    def slot(a, b):
-        k = 0 if topo.mates(a, b) else (1 if topo.same_plane(a, b) else 2)
-        return T.land[:, k * HALF:(k + 1) * HALF]
+    mate = [d for d in near if topo.mates(core, d)][0]
+    plane = [d for d in near if topo.same_plane(core, d)][0]
+    cross = [d for d in near if d not in (mate, plane)][0]
+    reach = [d for d in peers if d not in near and topo.may_write(core, d)]
+    cabled = [d for d in reach if topo.chip(d) == topo.chip(core)][0]
+    xcab = [d for d in reach if d != cabled][0]
+    slot = [T.land[:, k * HALF:(k + 1) * HALF] for k in range(4)]
 
     def dst_id(d):
         rid, pid = topo.addr(d, core)
         return DstId(rid=rid, pnc=pid)
 
-    def n_engines(mask):
-        return bin(mask).count("1")
+    mask = topo.mask(core, cabled)
+    for d in (mate, plane, cross, xcab):
+        mask &= topo.mask(core, d)
+    n = bin(mask).count("1")
 
-    mask1 = topo.mask(core, near[0]) & topo.mask(core, near[1]) & topo.mask(core, near[2])
-    mask2 = topo.mask(core, cabled)
+    def send(cores, sem, srcs, dsts, op):
+        g.remote_dma_fused([RemoteDMATransfer(
+            dst_ids=[dst_id(d) for d in cores], dma_engine_mask=mask, remote_sem=sem,
+            srcs=srcs, dsts=dsts, alu_op=op)], local_sem=S.snt)
 
     g.sync.dma_start(T.xs[:], T.x[:]).then_inc(S.ld, 16)
     g.scalar.dma_start(T.w[:, HALF:2 * HALF], T.v[:]).then_inc(S.ld, 16)
@@ -62,40 +67,40 @@ def rank_program(g, core, T, topo):
     g.vector.tensor_copy(T.p[:], T.pt[:, 0:HALF]).then_inc(S.pr, 1)
 
     g.wait_ge(S.pr, 1)
-    g.remote_dma_fused([RemoteDMATransfer(
-        dst_ids=[dst_id(d) for d in near], dma_engine_mask=mask1, remote_sem=S.a1,
-        srcs=[T.p[:]], dsts=[slot(core, d) for d in near], alu_op=0)], local_sem=S.snt)
+    send([cross, plane], S.a1, [T.p[:]], [slot[0], slot[1]], 0)
+    send([mate, xcab], S.ai, [T.p[:]], [slot[2], slot[3]], 0)
 
     g.vector.wait_ge(S.ldv, 32)
     g.vector.tensor_tensor(T.va[top, :], T.vraw[top, :], T.vraw[top, :], AluOpType.add).then_inc(S.vd, 1)
     g.vector.tensor_tensor(T.vb[bot, :], T.vraw[bot, :], T.vraw[bot, :], AluOpType.add).then_inc(S.vd, 1)
 
-    mine = [T.p[:]] + [slot(d, core) for d in near]
-    g.wait_ge(S.a1, 3 * n_engines(mask1))
-    g.remote_dma_fused([RemoteDMATransfer(
-        dst_ids=[dst_id(cabled)], dma_engine_mask=mask2, remote_sem=S.a2,
-        srcs=mine, dsts=[T.far[:]], alu_op=1)], local_sem=S.snt)
+    g.wait_ge(S.a1, 2 * n)
+    send([cabled], S.a2, [T.p[:], slot[0], slot[1]], [T.far[:]], 1)
 
+    halves = ((top, T.va, T.pe0, S.mf0), (bot, T.vb, T.pe1, S.mf1))
     g.tensor.wait_ge(S.pr, 1)
     g.tensor.wait_ge(S.zv, 2)
     g.tensor.wait_ge(S.vd, 2)
-    g.tensor.wait_ge(S.a1, 3 * n_engines(mask1))
-    for half, stat in ((top, T.va), (bot, T.vb)):
-        for i, src in enumerate(mine):
-            mm = g.tensor.matmul(T.pe[:, half], stat[:], src, i == 0, i == len(mine) - 1)
-        mm.then_inc(S.me, 1)
-    g.vector.wait_ge(S.ld, 32)
-    g.vector.wait_ge(S.me, 2)
-    g.vector.tensor_tensor(T.e[:], T.xs[:], T.pe[:, 0:2 * HALF], AluOpType.subtract).then_inc(S.ed, 1)
+    for _, stat, acc, _ in halves:
+        g.tensor.matmul(acc[:, 0:HALF], stat[:], T.p[:], True, False)
+    g.tensor.wait_ge(S.a1, 2 * n)
+    for _, stat, acc, _ in halves:
+        g.tensor.matmul(acc[:, 0:HALF], stat[:], slot[0], False, False)
+        g.tensor.matmul(acc[:, 0:HALF], stat[:], slot[1], False, False)
+    g.tensor.wait_ge(S.ai, 2 * n)
+    for _, stat, acc, _ in halves:
+        g.tensor.matmul(acc[:, 0:HALF], stat[:], slot[2], False, False)
+        g.tensor.matmul(acc[:, 0:HALF], stat[:], slot[3], False, False)
 
-    g.tensor.wait_ge(S.a2, n_engines(mask2))
-    for half, stat in ((top, T.va), (bot, T.vb)):
-        g.tensor.matmul(T.pf[:, half], stat[:], T.far[:], True, True).then_inc(S.mf, 1)
-    g.vector.wait_ge(S.ed, 1)
-    g.vector.wait_ge(S.mf, 2)
-    g.vector.tensor_tensor(T.ys[:], T.e[:], T.pf[:, 0:2 * HALF], AluOpType.subtract).then_inc(S.yr, 1)
-    g.sync.wait_ge(S.yr, 1)
+    g.tensor.wait_ge(S.a2, n)
+    for _, stat, acc, sem in halves:
+        g.tensor.matmul(acc[:, 0:HALF], stat[:], T.far[:], False, True).then_inc(sem, 1)
+    g.vector.wait_ge(S.ld, 32)
+    for half, _, acc, sem in halves:
+        g.vector.wait_ge(sem, 1)
+        g.vector.tensor_tensor(T.ys[:, half], T.xs[:, half], acc[:, 0:HALF], AluOpType.subtract).then_inc(S.yr, 1)
+    g.sync.wait_ge(S.yr, 2)
     g.sync.dma_start(T.y[:], T.ys[:]).then_inc(S.st, 16)
     g.sync.wait_ge(S.st, 16)
 
-    g.wait_ge(S.snt, n_engines(mask1) + n_engines(mask2))
+    g.wait_ge(S.snt, 3 * n)

from concourse.bass import DstId, RemoteDMATransfer
from concourse.mybir import AluOpType

HALF = 64

SCRATCH = {
    "xs": ("sbuf", [128, 128], "bfloat16"),
    "w": ("sbuf", [128, 192], "bfloat16"),
    "vraw": ("sbuf", [128, 128], "bfloat16"),
    "va": ("sbuf", [128, 128], "bfloat16"),
    "vb": ("sbuf", [128, 128], "bfloat16"),
    "p": ("sbuf", [128, HALF], "bfloat16"),
    "land": ("sbuf", [128, 4 * HALF], "bfloat16"),
    "far": ("sbuf", [128, HALF], "bfloat16"),
    "ys": ("sbuf", [128, 128], "bfloat16"),
    "pt": ("psum", [128, 512], "float32"),
    "pe0": ("psum", [128, 512], "float32"),
    "pe1": ("psum", [128, 512], "float32"),
}
SEMAPHORES = ["ld", "ldv", "z", "zv", "mt", "pr", "vd", "a1", "ai", "a2", "snt", "mf0", "mf1", "yr", "st"]


def rank_program(g, core, T, topo):
    if T.rank_of(core) is None:
        return
    S = T.sem
    top, bot = slice(0, HALF), slice(HALF, 2 * HALF)

    peers = [d for d in T.cores if d != core]
    near = [d for d in peers if topo.rack(topo.host(d)) == topo.rack(topo.host(core))]
    mate = [d for d in near if topo.mates(core, d)][0]
    plane = [d for d in near if topo.same_plane(core, d)][0]
    cross = [d for d in near if d not in (mate, plane)][0]
    reach = [d for d in peers if d not in near and topo.may_write(core, d)]
    cabled = [d for d in reach if topo.chip(d) == topo.chip(core)][0]
    xcab = [d for d in reach if d != cabled][0]
    slot = [T.land[:, k * HALF:(k + 1) * HALF] for k in range(4)]

    def dst_id(d):
        rid, pid = topo.addr(d, core)
        return DstId(rid=rid, pnc=pid)

    mask = topo.mask(core, cabled)
    for d in (mate, plane, cross, xcab):
        mask &= topo.mask(core, d)
    n = bin(mask).count("1")

    def send(cores, sem, srcs, dsts, op):
        g.remote_dma_fused([RemoteDMATransfer(
            dst_ids=[dst_id(d) for d in cores], dma_engine_mask=mask, remote_sem=sem,
            srcs=srcs, dsts=dsts, alu_op=op)], local_sem=S.snt)

    g.sync.dma_start(T.xs[:], T.x[:]).then_inc(S.ld, 16)
    g.scalar.dma_start(T.w[:, HALF:2 * HALF], T.v[:]).then_inc(S.ld, 16)
    g.sync.dma_start(T.vraw[top, :], T.vt[:]).then_inc(S.ldv, 16)
    g.scalar.dma_start(T.vraw[bot, :], T.vt[:]).then_inc(S.ldv, 16)
    g.vector.memset(T.w[:, 0:HALF], 0.0).then_inc(S.z, 1)
    g.vector.memset(T.w[:, 2 * HALF:3 * HALF], 0.0).then_inc(S.z, 1)
    g.vector.memset(T.va[bot, :], 0.0).then_inc(S.zv, 1)
    g.vector.memset(T.vb[top, :], 0.0).then_inc(S.zv, 1)

    g.tensor.wait_ge(S.z, 2)
    g.tensor.wait_ge(S.ld, 32)
    g.tensor.matmul(T.pt[:, 0:HALF], T.w[:, HALF:3 * HALF], T.xs[:, top], True, False)
    g.tensor.matmul(T.pt[:, 0:HALF], T.w[:, 0:2 * HALF], T.xs[:, bot], False, True).then_inc(S.mt, 1)
    g.vector.wait_ge(S.mt, 1)
    g.vector.tensor_copy(T.p[:], T.pt[:, 0:HALF]).then_inc(S.pr, 1)

    g.wait_ge(S.pr, 1)
    send([cross, plane], S.a1, [T.p[:]], [slot[0], slot[1]], 0)
    send([mate, xcab], S.ai, [T.p[:]], [slot[2], slot[3]], 0)

    g.vector.wait_ge(S.ldv, 32)
    g.vector.tensor_tensor(T.va[top, :], T.vraw[top, :], T.vraw[top, :], AluOpType.add).then_inc(S.vd, 1)
    g.vector.tensor_tensor(T.vb[bot, :], T.vraw[bot, :], T.vraw[bot, :], AluOpType.add).then_inc(S.vd, 1)

    g.wait_ge(S.a1, 2 * n)
    send([cabled], S.a2, [T.p[:], slot[0], slot[1]], [T.far[:]], 1)

    halves = ((top, T.va, T.pe0, S.mf0), (bot, T.vb, T.pe1, S.mf1))
    g.tensor.wait_ge(S.pr, 1)
    g.tensor.wait_ge(S.zv, 2)
    g.tensor.wait_ge(S.vd, 2)
    for _, stat, acc, _ in halves:
        g.tensor.matmul(acc[:, 0:HALF], stat[:], T.p[:], True, False)
    g.tensor.wait_ge(S.a1, 2 * n)
    for _, stat, acc, _ in halves:
        g.tensor.matmul(acc[:, 0:HALF], stat[:], slot[0], False, False)
        g.tensor.matmul(acc[:, 0:HALF], stat[:], slot[1], False, False)
    g.tensor.wait_ge(S.ai, 2 * n)
    for _, stat, acc, _ in halves:
        g.tensor.matmul(acc[:, 0:HALF], stat[:], slot[2], False, False)
        g.tensor.matmul(acc[:, 0:HALF], stat[:], slot[3], False, False)

    g.tensor.wait_ge(S.a2, n)
    for _, stat, acc, sem in halves:
        g.tensor.matmul(acc[:, 0:HALF], stat[:], T.far[:], False, True).then_inc(sem, 1)
    g.vector.wait_ge(S.ld, 32)
    for half, _, acc, sem in halves:
        g.vector.wait_ge(sem, 1)
        g.vector.tensor_tensor(T.ys[:, half], T.xs[:, half], acc[:, 0:HALF], AluOpType.subtract).then_inc(S.yr, 1)
    g.sync.wait_ge(S.yr, 2)
    g.sync.dma_start(T.y[:], T.ys[:]).then_inc(S.st, 16)
    g.sync.wait_ge(S.st, 16)

    g.wait_ge(S.snt, 3 * n)
